import numpy as np
import ml_dtypes


def mxq(x, axis, fmt="e4m3"):
    dtype, down = {"e4m3": (ml_dtypes.float8_e4m3fn, 7), "e5m2": (ml_dtypes.float8_e5m2, 14)}[fmt]
    v = np.moveaxis(np.asarray(x, np.float32).astype(ml_dtypes.bfloat16).astype(np.float64), axis, -1)
    blocks = v.reshape(v.shape[:-1] + (-1, 32))
    amax = np.abs(blocks).max(-1, keepdims=True)
    byte = np.maximum(np.where(amax > 0, np.frexp(amax)[1] - 1 + 127, 0) - down, 1)
    scale = np.exp2(byte - 127.0)
    codes = (blocks / scale).astype(np.float32).astype(dtype).astype(np.float64)
    return np.moveaxis((codes * scale).reshape(v.shape), -1, axis)


WIDE = False


def mx_kscale(k):
    if not WIDE:
        return np.ones(k)
    levels = np.array([10, -10, 5, -5, 0])
    if k % 512:
        return np.exp2(np.random.permutation(np.resize(levels, k // 32))).repeat(32)
    a = np.empty((k // 512, 16))
    for p in range(k // 512):
        a[p, :8] = np.random.permutation(np.resize(levels, 8))
        for g in range(8):
            far = levels[np.abs(levels - a[p, g]) >= 10]
            a[p, g + 8] = far[np.random.randint(len(far))]
    return np.exp2(a.ravel()).repeat(32)


def f64(x):
    return np.asarray(x).astype(np.float64)


def striped(idx):
    return np.tile(idx.reshape(-1, 16).T, (8, 1)).astype(np.uint16)


def unstriped(offs):
    return offs[:16].T.reshape(-1).astype(np.int64)


E2M1 = np.array([0.0, 0.5, 1.0, 1.5, 2.0, 3.0, 4.0, 6.0, -0.0, -0.5, -1.0, -1.5, -2.0, -3.0, -4.0, -6.0])


def pack_weight(w, fmt):
    k, n = w.shape
    w = f64(np.asarray(w, np.float32).astype(ml_dtypes.bfloat16)).reshape(k // 32, 32, n)
    amax = np.abs(w).max(1)
    if fmt == "e4m3":
        byte = np.frexp(amax)[1] - 1 + 127 - 7
    else:
        mant, ex = np.frexp(amax / 6.0)
        byte = np.where(mant > 0.5, ex, ex - 1) + 127
    byte = np.clip(np.where(amax > 0, byte, 1), 1, 254)
    scaled = (w * np.exp2(127.0 - byte)[:, None, :]).reshape(k, n).astype(np.float32)
    by_word = np.ascontiguousarray(scaled.reshape(k // 512, 128, 4, n).transpose(0, 1, 3, 2))
    if fmt == "e4m3":
        words = by_word.astype(ml_dtypes.float8_e4m3fn).view(np.uint8)
    else:
        c = by_word.astype(ml_dtypes.float4_e2m1fn).view(np.uint8) & 0xF
        words = (c[..., 0::2] | (c[..., 1::2] << 4)).reshape(k // 512, 128, 2 * n)
    return np.ascontiguousarray(words), np.ascontiguousarray(byte.astype(np.uint8).reshape(k // 512, 16, n))


def unpack_weight(words, scales, fmt):
    g, _, n = scales.shape
    words = np.ascontiguousarray(words).reshape(g, 128, n, -1)
    if fmt == "e4m3":
        vals = words.view(ml_dtypes.float8_e4m3fn).astype(np.float64)
    else:
        nib = np.empty((g, 128, n, 4), np.uint8)
        nib[..., 0::2] = words & 0xF
        nib[..., 1::2] = words >> 4
        vals = E2M1[nib]
    vals = vals * np.repeat(np.exp2(scales.astype(np.float64) - 127.0), 8, axis=1)[..., None]
    return vals.transpose(0, 1, 3, 2).reshape(g * 512, n)


def gelu(v):
    return 0.5 * v * (1.0 + np.tanh(np.sqrt(2.0 / np.pi) * (v + 0.044715 * v**3)))


def striped8(idx):
    return np.concatenate([v.reshape(-1, 16).T for v in idx]).astype(np.uint16)


def unstriped8(offs):
    return np.stack([offs[16 * g:16 * g + 16].T.reshape(-1) for g in range(8)]).astype(np.int64)


def runs(v, idx8):
    k = np.arange(v.shape[0])
    return v[k[:, None], idx8[k % 512 // 64]]


K, H, N, T, S, P, R, C = 1536, 1024, 512, 4096, 1024, 512, 8, 64

def setup_inputs():
    n = np.random.standard_normal
    s = mx_kscale(K)[:, None]
    u = mx_kscale(H)[:, None]
    tab_words, tab_scales = pack_weight(n((K, T)) * s, "e4m3")
    w4_words, w4_scales = pack_weight(n((H, N)) / np.sqrt(H) / u, "e2m1")
    orders = np.stack([np.random.permutation(S)[:P] for _ in range(R)])
    return {
        "tab_words": tab_words, "tab_scales": tab_scales,
        "w1": (0.7 * n((K, H)) / np.sqrt(K) / s).astype(np.float32),
        "b1": (0.6 * n(H)).astype(np.float32),
        "sc": np.repeat(np.random.uniform(0.6, 3.0, H // C), C).astype(np.float32),
        "th": np.repeat(n(H // C), C).astype(np.float32),
        "base": np.random.uniform(0.15, 0.5, H).astype(np.float32),
        "gain": (np.random.choice([-1.0, 1.0], H) * np.random.uniform(0.6, 2.0, H) * u[:, 0]).astype(np.float32),
        "w4_words": w4_words, "w4_scales": w4_scales,
        "ov": np.random.uniform(0.4, 1.6, N).astype(np.float32),
        "offs": striped(np.random.permutation(T)[:S]),
        "offs2": striped8(orders),
    }

def reference(tab_words, tab_scales, w1, b1, sc, th, base, gain, w4_words, w4_scales, ov, offs, offs2):
    v = unpack_weight(tab_words, tab_scales, "e4m3")[:, unstriped(offs)]
    h = (mxq(f64(w1), 0, "e4m3").T @ v) + f64(b1)[:, None]
    hp = runs(h, unstriped8(offs2))
    a = 1.0 / (1.0 + np.exp(-(f64(sc)[:, None] * hp + f64(th)[:, None])))
    load = f64(base) + a.sum(axis=1) / P
    y = hp / load[:, None] * f64(gain)[:, None]
    z = unpack_weight(w4_words, w4_scales, "e2m1").T @ mxq(y, 0, "e4m3")
    return z * f64(ov)[:, None]

@@ -1,0 +1,347 @@
+from contextlib import ExitStack
+
+import concourse.mybir as mybir
+from concourse.masks import make_identity
+
+F32 = mybir.dt.float32
+BF16 = mybir.dt.bfloat16
+I32 = mybir.dt.int32
+U32 = mybir.dt.uint32
+U16 = mybir.dt.uint16
+U8 = mybir.dt.uint8
+FP8X4 = mybir.dt.float8_e4m3fn_x4
+FP4X4 = mybir.dt.float4_e2m1fn_x4
+ACT = mybir.ActivationFunctionType
+ALU = mybir.AluOpType
+
+K, H, N, T, S, M = 1536, 1024, 512, 4096, 1024, 512
+P = 128
+PACK = 4
+SPAN = P * PACK
+K_PASSES = K // SPAN
+H_PASSES = H // SPAN
+BANK = 512
+HALF = M // 2
+
+FLOPS = 2 * K * H * S + 2 * H * N * M
+
+SCALAR_EVAC = [(0, 3), (1, 3)]
+
+
+def tile_list_echo_load_traits_kernel(
+    tc, tab_words, tab_scales, w1, b1, sc, th, base, gain, w4_words, w4_scales, ov, offs, offs2, out
+):
+    nc = tc.nc
+    with ExitStack() as ctx:
+        keep = ctx.enter_context(tc.tile_pool(name="keep", bufs=1))
+        ring = ctx.enter_context(tc.tile_pool(name="ring", bufs=3))
+        psum = ctx.enter_context(tc.psum_pool(name="psum", bufs=1))
+
+        def bank(n, shape):
+            return psum.tile(shape, F32, name="bank%d" % n, tag="bank%d" % n)
+
+        idx = keep.tile([P, S // 16], U16, name="idx")
+        nc.sync.dma_start(idx[:], offs)
+
+        tab_sc = keep.tile([P, T], U8, name="tab_sc", align_bytes=64)
+        nc.vector.memset(tab_sc[:].bitcast(I32), 0)
+        rows = keep.tile([P, SPAN], F32, name="rows")
+        nc.vector.memset(rows[:], 0.0)
+        w4_sc = keep.tile([P, H_PASSES, N], U8, name="w4_sc", align_bytes=64)
+        nc.vector.memset(w4_sc[:].bitcast(I32), 0)
+
+        ident = keep.tile([P, P], F32, name="ident")
+        make_identity(nc, ident[:])
+        for q in range(4):
+            nc.gpsimd.dma_start(
+                tab_sc[32 * q : 32 * q + 4 * K_PASSES, :].bitcast(I32),
+                tab_scales[:, 4 * q : 4 * q + 4, :].bitcast(I32),
+            )
+
+        vecs = [b1, sc, th, base, gain]
+        for v, vec in enumerate(vecs):
+            nc.scalar.dma_start(
+                rows[H_PASSES * v : H_PASSES * (v + 1), :], vec.rearrange("(b c) -> b c", b=H_PASSES)
+            )
+        nc.scalar.dma_start(rows[16:20, 0:P], ov.rearrange("(c p) -> c p", p=P))
+
+        tab = []
+        raw = {}
+
+        def load_tab(a):
+            t = keep.tile([P, T], I32, name="tab%d" % a)
+            nc.sync.dma_start(t[:], tab_words[a].rearrange("p t i -> p (t i)").bitcast(I32))
+            tab.append(t)
+
+        def load_w1(b, a):
+            t = keep.tile([P, PACK, SPAN], F32, name="raw%d%d" % (b, a), tag="raw%d%d" % (b, a))
+            nc.sync.dma_start(
+                t[:],
+                w1[a * SPAN : (a + 1) * SPAN, b * SPAN : (b + 1) * SPAN].rearrange("(p j) c -> p j c", j=PACK),
+            )
+            raw[b, a] = t
+
+        for a in range(K_PASSES):
+            load_tab(a)
+            load_w1(0, a)
+        idx2 = keep.tile([P, M // 16], U16, name="idx2")
+        nc.sync.dma_start(idx2[:], offs2)
+        for a in range(K_PASSES):
+            load_w1(1, a)
+        w4 = keep.tile([P, H_PASSES, 2 * N], U8, name="w4", align_bytes=64)
+        nc.sync.dma_start(w4[:].bitcast(I32), w4_words.rearrange("a p n -> p a n").bitcast(I32))
+
+        for q in range(4):
+            nc.sync.dma_start(
+                w4_sc[32 * q : 32 * q + 4, :, :].bitcast(I32),
+                w4_scales[:, 4 * q : 4 * q + 4, :].rearrange("a r n -> r a n").bitcast(I32),
+            )
+
+        turned = bank(0, [P, PACK, P])
+        for i in range(PACK):
+            nc.tensor.transpose(turned[:, i, :], rows[:, i:SPAN:PACK], ident[:])
+        turned_ov = bank(1, [P, P])
+        nc.tensor.transpose(turned_ov[:], rows[:, 0:P], ident[:])
+        n_rows = H_PASSES * len(vecs)
+        cols = keep.tile([P, n_rows * PACK], F32, name="cols")
+        nc.vector.tensor_copy(cols[:].rearrange("p (r i) -> p i r", i=PACK), turned[:, :, 0:n_rows])
+        ov_cols = keep.tile([P, 4], F32, name="ov_cols")
+        nc.vector.tensor_copy(ov_cols[:], turned_ov[:, 16:20])
+
+        def col(v, b, i0, i1):
+            c = (H_PASSES * v + b) * PACK
+            return cols[:, c + i0 : c + i1]
+
+        v_sc = keep.tile([P, S], U8, name="v_sc", align_bytes=64)
+        v_words = []
+
+        def gather_tab(a):
+            t = keep.tile([P, S], U32, name="v%d" % a, align_bytes=64)
+            nc.vector.tensor_copy(t[:], tab[a][:].bitcast(U32).indirect(idx[:]))
+            v_words.append(t)
+
+        w_bf = {}
+        w_codes = {}
+        w_sc = {}
+
+        def weave_w1(engine_copy, b, a, i0, i1):
+            if (b, a) not in w_bf:
+                w_bf[b, a] = ring.tile([P, PACK, P, PACK], BF16, name="w_bf", align_bytes=64)
+                w_codes[b, a] = keep.tile([P, SPAN], U32, name="wc%d%d" % (b, a), align_bytes=64)
+                w_sc[b, a] = keep.tile([P, SPAN], U8, name="ws%d%d" % (b, a), align_bytes=64)
+            engine_copy(
+                w_bf[b, a][:, i0:i1, :, :].rearrange("p i m j -> p m j i"),
+                raw[b, a][:].rearrange("p j (m i) -> p m j i", i=PACK)[:, :, :, i0:i1],
+            )
+
+        def quant_w1(b, a, i0, i1):
+            nc.vector.quantize_mx(
+                out=w_codes[b, a][:, i0 * P : i1 * P].bitcast(FP8X4),
+                scales=w_sc[b, a][:, i0 * P : i1 * P],
+                in_=w_bf[b, a][:, i0:i1, :, :].rearrange("p i m j -> p (i m j)"),
+            )
+
+        acc_banks = {}
+
+        def mm1(b, a, i):
+            for u in range(2):
+                if a == 0:
+                    acc_banks[b, i, u] = bank(2 * i + u, [P, BANK])
+                nc.tensor.matmul_mx(
+                    out=acc_banks[b, i, u][:],
+                    lhsT=w_codes[b, a][:, i * P : (i + 1) * P].bitcast(FP8X4),
+                    lhsT_scale=w_sc[b, a][:, i * P : (i + 1) * P],
+                    rhs=v_words[a][:, u * BANK : (u + 1) * BANK].bitcast(FP8X4),
+                    rhs_scale=v_sc[4 * a : P, u * BANK : (u + 1) * BANK],
+                    start=(a == 0),
+                    stop=(a == K_PASSES - 1),
+                )
+
+        h = {}
+
+        def evac(b, i):
+            h[b, i] = keep.tile([P, S], F32, name="h%d%d" % (b, i))
+            for u in range(2):
+                dst = h[b, i][:, u * BANK : (u + 1) * BANK]
+                if (b, i) in SCALAR_EVAC:
+                    nc.scalar.activation(dst, acc_banks[b, i, u][:], ACT.Identity, bias=col(0, b, i, i + 1))
+                else:
+                    nc.vector.tensor_scalar(dst, acc_banks[b, i, u][:], col(0, b, i, i + 1), None, ALU.add)
+
+        sums = [keep.tile([P, PACK], F32, name="sums%d" % b) for b in range(H_PASSES)]
+        picked = [keep.tile([P, PACK, M], F32, name="picked%d" % b, tag="raw0%d" % b) for b in range(H_PASSES)]
+
+        openings = {}
+
+        def look(b, i):
+            opening = ring.tile([P, M], F32, name="opening", bufs=6)
+            nc.scalar.activation(
+                opening[:],
+                h[b, i][:].indirect(idx2[:]),
+                ACT.Sigmoid,
+                bias=col(2, b, i, i + 1),
+                scale=col(1, b, i, i + 1),
+            )
+            openings[b, i] = opening
+
+        pair_sums = {}
+
+        def row_sum(b, i):
+            if b not in pair_sums:
+                pair_sums[b] = keep.tile([P, PACK, HALF], F32, name="pair_sums%d" % b, tag="raw1%d" % (2 - b))
+            nc.vector.scalar_tensor_tensor(
+                pair_sums[b][:, i, :],
+                openings[b, i][:, 0:HALF],
+                1.0,
+                openings[b, i][:, HALF:M],
+                ALU.mult,
+                ALU.add,
+                accum_out=sums[b][:, i : i + 1],
+            )
+
+        def pick(b, i, m0, m1):
+            nc.scalar.activation(
+                picked[b][:, i, m0:m1], h[b, i][:].indirect(idx2[:, m0 // 16 : m1 // 16]), ACT.Copy
+            )
+
+        factor = {}
+
+        def make_factor(b):
+            load = keep.tile([P, PACK], F32, name="load%d" % b)
+            nc.vector.scalar_tensor_tensor(load[:], sums[b][:], 1.0 / M, col(3, b, 0, PACK), ALU.mult, ALU.add)
+            inv = keep.tile([P, PACK], F32, name="inv%d" % b)
+            nc.vector.reciprocal(inv[:], load[:])
+            factor[b] = keep.tile([P, PACK], F32, name="factor%d" % b)
+            nc.vector.tensor_tensor(factor[b][:], inv[:], col(4, b, 0, PACK), ALU.mult)
+
+        y_rows = [keep.tile([P, PACK, M], BF16, name="y_rows%d" % b) for b in range(H_PASSES)]
+        y_bf = [keep.tile([P, M, PACK], BF16, name="y_bf%d" % b, align_bytes=64) for b in range(H_PASSES)]
+        y_codes = [keep.tile([P, M], U32, name="y_codes%d" % b, align_bytes=64) for b in range(H_PASSES)]
+        y_sc = [keep.tile([P, M], U8, name="y_sc%d" % b, align_bytes=64) for b in range(H_PASSES)]
+
+        def scale_y(b, i, m0, m1):
+            nc.vector.tensor_scalar(
+                y_rows[b][:, i, m0:m1], picked[b][:, i, m0:m1], factor[b][:, i : i + 1], None, ALU.mult
+            )
+
+        def weave_y(b, m0, m1):
+            nc.vector.tensor_copy(
+                y_bf[b][:, m0:m1, :].rearrange("p (c u) i -> p c i u", u=4),
+                y_rows[b][:, :, m0:m1].rearrange("p i (c u) -> p c i u", u=4),
+            )
+
+        def quant_y(b, m0, m1):
+            nc.vector.quantize_mx(
+                out=y_codes[b][:, m0:m1].bitcast(FP8X4),
+                scales=y_sc[b][:, m0:m1],
+                in_=y_bf[b][:, m0:m1, :].rearrange("p m i -> p (m i)"),
+            )
+
+        z_banks = {}
+
+        def mm2(b, u):
+            for c in range(4):
+                if b == 0:
+                    z_banks[u, c] = bank(4 * u + c, [P, HALF])
+                nc.tensor.matmul_mx(
+                    out=z_banks[u, c][:],
+                    lhsT=w4[:, b, 2 * P * c : 2 * P * (c + 1)].bitcast(FP4X4),
+                    lhsT_scale=w4_sc[:, b, P * c : P * (c + 1)],
+                    rhs=y_codes[b][:, u * HALF : (u + 1) * HALF].bitcast(FP8X4),
+                    rhs_scale=y_sc[b][:, u * HALF : (u + 1) * HALF],
+                    start=(b == 0),
+                    stop=(b == H_PASSES - 1),
+                )
+
+        out_v = out.rearrange("(c p) m -> p c m", p=P)
+
+        def finish(u, scalar_share):
+            for g in range(2):
+                res = keep.tile([P, 2, HALF], F32, name="res%d%d" % (u, g))
+                for e in range(2):
+                    c = 2 * g + e
+                    if g == 1 and scalar_share:
+                        nc.scalar.activation(
+                            res[:, e, :], z_banks[u, c][:], ACT.Copy, scale=ov_cols[:, c : c + 1]
+                        )
+                    else:
+                        nc.vector.tensor_scalar(
+                            res[:, e, :], z_banks[u, c][:], ov_cols[:, c : c + 1], None, ALU.mult
+                        )
+                nc.sync.dma_start(out_v[:, 2 * g : 2 * g + 2, u * HALF : (u + 1) * HALF], res[:])
+
+        gather_tab(0)
+        nc.vector.tensor_copy(v_sc[:], tab_sc[:].indirect(idx[:]))
+        for a in range(K_PASSES - 1):
+            if a > 0:
+                gather_tab(a)
+            weave_w1(nc.scalar.copy, 0, a, 0, PACK)
+            quant_w1(0, a, 0, PACK)
+            for i in range(PACK):
+                mm1(0, a, i)
+        last = K_PASSES - 1
+        gather_tab(last)
+        weave_w1(nc.vector.tensor_copy, 0, last, 0, 2)
+        quant_w1(0, last, 0, 2)
+        mm1(0, last, 0)
+        mm1(0, last, 1)
+        weave_w1(nc.vector.tensor_copy, 0, last, 2, 4)
+        evac(0, 0)
+        look(0, 0)
+        quant_w1(0, last, 2, 4)
+        mm1(0, last, 2)
+        mm1(0, last, 3)
+        evac(0, 1)
+        pick(0, 0, 0, M)
+        look(0, 1)
+        pick(0, 1, 0, M)
+        weave_w1(nc.vector.tensor_copy, 1, 0, 0, PACK)
+        evac(0, 2)
+        quant_w1(1, 0, 0, PACK)
+        look(0, 2)
+        pick(0, 2, 0, M)
+        evac(0, 3)
+        look(0, 3)
+        pick(0, 3, 0, M)
+        weave_w1(nc.vector.tensor_copy, 1, 1, 0, PACK)
+        quant_w1(1, 1, 0, PACK)
+        weave_w1(nc.vector.tensor_copy, 1, 2, 0, PACK)
+        quant_w1(1, 2, 0, PACK)
+        for i in range(PACK):
+            for a in range(K_PASSES):
+                mm1(1, a, i)
+        evac(1, 0)
+        look(1, 0)
+        pick(1, 0, 0, M)
+        evac(1, 1)
+        look(1, 1)
+        pick(1, 1, 0, M)
+        for i in range(PACK):
+            row_sum(0, i)
+        evac(1, 2)
+        make_factor(0)
+        look(1, 2)
+        evac(1, 3)
+        look(1, 3)
+        for i in range(PACK):
+            scale_y(0, i, 0, M)
+        weave_y(0, 0, M)
+        for i in range(PACK):
+            row_sum(1, i)
+        quant_y(0, 0, M)
+        mm2(0, 0)
+        mm2(0, 1)
+        make_factor(1)
+        for u in range(2):
+            pick(1, 2, u * HALF, (u + 1) * HALF)
+            pick(1, 3, u * HALF, (u + 1) * HALF)
+        scale_y(1, 0, 0, M)
+        scale_y(1, 1, 0, M)
+        for u in range(2):
+            scale_y(1, 2, u * HALF, (u + 1) * HALF)
+            scale_y(1, 3, u * HALF, (u + 1) * HALF)
+            weave_y(1, u * HALF, (u + 1) * HALF)
+            quant_y(1, u * HALF, (u + 1) * HALF)
+            mm2(1, u)
+        finish(0, True)
+        finish(1, True)

@@ -25,7 +25,7 @@ HALF = M // 2
 
 FLOPS = 2 * K * H * S + 2 * H * N * M
 
-SCALAR_EVAC = [(0, 3), (1, 3)]
+SCALAR_EVAC = [(0, 3)]
 
 
 def tile_list_echo_load_traits_kernel(
@@ -105,6 +105,8 @@ def tile_list_echo_load_traits_kernel(
         n_rows = H_PASSES * len(vecs)
         cols = keep.tile([P, n_rows * PACK], F32, name="cols")
         nc.vector.tensor_copy(cols[:].rearrange("p (r i) -> p i r", i=PACK), turned[:, :, 0:n_rows])
+        last_cols = keep.tile([P, 2], F32, name="last_cols", tag="late")
+        nc.vector.tensor_copy(last_cols[:], turned[:, PACK - 1, 3:6:2])
         ov_cols = keep.tile([P, 4], F32, name="ov_cols")
         nc.vector.tensor_copy(ov_cols[:], turned_ov[:, 16:20])
 
@@ -169,18 +171,28 @@ def tile_list_echo_load_traits_kernel(
                     nc.vector.tensor_scalar(dst, acc_banks[b, i, u][:], col(0, b, i, i + 1), None, ALU.add)
 
         sums = [keep.tile([P, PACK], F32, name="sums%d" % b) for b in range(H_PASSES)]
-        picked = [keep.tile([P, PACK, M], F32, name="picked%d" % b, tag="raw0%d" % b) for b in range(H_PASSES)]
+        picked0 = keep.tile([P, PACK, M], F32, name="picked0", tag="raw00")
+        picked1 = [
+            keep.tile([P, PACK, HALF], F32, name="picked10", tag="raw01"),
+            keep.tile([P, PACK, HALF], F32, name="picked11", tag="late"),
+        ]
+
+        def picked(b, i, m0, m1):
+            if b == 0:
+                return picked0[:, i, m0:m1]
+            return picked1[m0 // HALF][:, i, :]
+
 
         openings = {}
 
         def look(b, i):
-            opening = ring.tile([P, M], F32, name="opening", bufs=6)
+            opening = ring.tile([P, M], F32, name="opening", bufs=8)
             nc.scalar.activation(
                 opening[:],
                 h[b, i][:].indirect(idx2[:]),
                 ACT.Sigmoid,
-                bias=col(2, b, i, i + 1),
-                scale=col(1, b, i, i + 1),
+                bias=last_cols[:, 1:2] if (b, i) == (1, 3) else col(2, b, i, i + 1),
+                scale=last_cols[:, 0:1] if (b, i) == (1, 3) else col(1, b, i, i + 1),
             )
             openings[b, i] = opening
 
@@ -201,7 +213,7 @@ def tile_list_echo_load_traits_kernel(
 
         def pick(b, i, m0, m1):
             nc.scalar.activation(
-                picked[b][:, i, m0:m1], h[b, i][:].indirect(idx2[:, m0 // 16 : m1 // 16]), ACT.Copy
+                picked(b, i, m0, m1), h[b, i][:].indirect(idx2[:, m0 // 16 : m1 // 16]), ACT.Copy
             )
 
         factor = {}
@@ -221,7 +233,17 @@ def tile_list_echo_load_traits_kernel(
 
         def scale_y(b, i, m0, m1):
             nc.vector.tensor_scalar(
-                y_rows[b][:, i, m0:m1], picked[b][:, i, m0:m1], factor[b][:, i : i + 1], None, ALU.mult
+                y_rows[b][:, i, m0:m1], picked(b, i, m0, m1), factor[b][:, i : i + 1], None, ALU.mult
+            )
+
+        def scale_y_pool(b, i):
+            nc.gpsimd.tensor_scalar(
+                y_rows[b][:, i, :], picked(b, i, 0, M), factor[b][:, i : i + 1], 0.0, ALU.mult, ALU.add
+            )
+
+        def scale_y_scalar(b, i, m0, m1):
+            nc.scalar.activation(
+                y_rows[b][:, i, m0:m1], picked(b, i, m0, m1), ACT.Copy, scale=factor[b][:, i : i + 1]
             )
 
         def weave_y(b, m0, m1):
@@ -255,20 +277,14 @@ def tile_list_echo_load_traits_kernel(
 
         out_v = out.rearrange("(c p) m -> p c m", p=P)
 
-        def finish(u, scalar_share):
-            for g in range(2):
-                res = keep.tile([P, 2, HALF], F32, name="res%d%d" % (u, g))
-                for e in range(2):
-                    c = 2 * g + e
-                    if g == 1 and scalar_share:
-                        nc.scalar.activation(
-                            res[:, e, :], z_banks[u, c][:], ACT.Copy, scale=ov_cols[:, c : c + 1]
-                        )
-                    else:
-                        nc.vector.tensor_scalar(
-                            res[:, e, :], z_banks[u, c][:], ov_cols[:, c : c + 1], None, ALU.mult
-                        )
-                nc.sync.dma_start(out_v[:, 2 * g : 2 * g + 2, u * HALF : (u + 1) * HALF], res[:])
+        def finish(u, on_scalar):
+            for c in range(4):
+                res = keep.tile([P, HALF], F32, name="res%d%d" % (u, c))
+                if c in on_scalar:
+                    nc.scalar.activation(res[:], z_banks[u, c][:], ACT.Copy, scale=ov_cols[:, c : c + 1])
+                else:
+                    nc.vector.tensor_scalar(res[:], z_banks[u, c][:], ov_cols[:, c : c + 1], None, ALU.mult)
+                nc.sync.dma_start(out_v[:, c, u * HALF : (u + 1) * HALF], res[:])
 
         gather_tab(0)
         nc.vector.tensor_copy(v_sc[:], tab_sc[:].indirect(idx[:]))
@@ -282,66 +298,75 @@ def tile_list_echo_load_traits_kernel(
         last = K_PASSES - 1
         gather_tab(last)
         weave_w1(nc.vector.tensor_copy, 0, last, 0, 2)
+        weave_w1(nc.scalar.copy, 0, last, 2, 4)
         quant_w1(0, last, 0, 2)
         mm1(0, last, 0)
         mm1(0, last, 1)
-        weave_w1(nc.vector.tensor_copy, 0, last, 2, 4)
-        evac(0, 0)
-        look(0, 0)
         quant_w1(0, last, 2, 4)
         mm1(0, last, 2)
         mm1(0, last, 3)
+        evac(0, 0)
+        look(0, 0)
         evac(0, 1)
         pick(0, 0, 0, M)
+        weave_w1(nc.vector.tensor_copy, 1, 0, 0, PACK)
         look(0, 1)
         pick(0, 1, 0, M)
-        weave_w1(nc.vector.tensor_copy, 1, 0, 0, PACK)
         evac(0, 2)
         quant_w1(1, 0, 0, PACK)
+        weave_w1(nc.vector.tensor_copy, 1, 1, 0, PACK)
         look(0, 2)
         pick(0, 2, 0, M)
+        quant_w1(1, 1, 0, PACK)
+        for i in range(2):
+            for a in range(last):
+                mm1(1, a, i)
+        weave_w1(nc.vector.tensor_copy, 1, last, 0, PACK)
         evac(0, 3)
         look(0, 3)
         pick(0, 3, 0, M)
-        weave_w1(nc.vector.tensor_copy, 1, 1, 0, PACK)
-        quant_w1(1, 1, 0, PACK)
-        weave_w1(nc.vector.tensor_copy, 1, 2, 0, PACK)
-        quant_w1(1, 2, 0, PACK)
-        for i in range(PACK):
+        quant_w1(1, last, 0, 2)
+        mm1(1, last, 0)
+        mm1(1, last, 1)
+        quant_w1(1, last, 2, 4)
+        for i in range(2, PACK):
             for a in range(K_PASSES):
                 mm1(1, a, i)
+        for i in range(PACK - 1):
+            row_sum(0, i)
         evac(1, 0)
         look(1, 0)
-        pick(1, 0, 0, M)
-        evac(1, 1)
-        look(1, 1)
-        pick(1, 1, 0, M)
-        for i in range(PACK):
-            row_sum(0, i)
-        evac(1, 2)
+        pick(1, 0, 0, HALF)
+        row_sum(0, PACK - 1)
         make_factor(0)
-        look(1, 2)
-        evac(1, 3)
-        look(1, 3)
         for i in range(PACK):
-            scale_y(0, i, 0, M)
+            scale_y_pool(0, i)
+        for i in range(1, PACK):
+            evac(1, i)
+            look(1, i)
+            pick(1, i, 0, HALF)
+        for i in range(PACK):
+            pick(1, i, HALF, M)
+        row_sum(1, 0)
         weave_y(0, 0, M)
-        for i in range(PACK):
-            row_sum(1, i)
+        row_sum(1, 1)
         quant_y(0, 0, M)
+        for i in range(2, PACK):
+            row_sum(1, i)
         mm2(0, 0)
         mm2(0, 1)
         make_factor(1)
-        for u in range(2):
-            pick(1, 2, u * HALF, (u + 1) * HALF)
-            pick(1, 3, u * HALF, (u + 1) * HALF)
-        scale_y(1, 0, 0, M)
-        scale_y(1, 1, 0, M)
-        for u in range(2):
-            scale_y(1, 2, u * HALF, (u + 1) * HALF)
-            scale_y(1, 3, u * HALF, (u + 1) * HALF)
-            weave_y(1, u * HALF, (u + 1) * HALF)
-            quant_y(1, u * HALF, (u + 1) * HALF)
-            mm2(1, u)
-        finish(0, True)
-        finish(1, True)
+        for i in range(PACK):
+            scale_y(1, i, 0, HALF)
+        weave_y(1, 0, HALF)
+        scale_y(1, 0, HALF, M)
+        quant_y(1, 0, HALF)
+        mm2(1, 0)
+        scale_y(1, 1, HALF, M)
+        scale_y_scalar(1, 2, HALF, M)
+        scale_y_scalar(1, 3, HALF, M)
+        weave_y(1, HALF, M)
+        quant_y(1, HALF, M)
+        mm2(1, 1)
+        finish(0, [0, 1, 2, 3])
+        finish(1, [1, 3])

@@ -25,7 +25,8 @@ HALF = M // 2
 
 FLOPS = 2 * K * H * S + 2 * H * N * M
 
-SCALAR_EVAC = [(0, 3)]
+SCALAR_EVAC = [(0, 3, 0), (0, 3, 1)]
+ROW = M + 2
 
 
 def tile_list_echo_load_traits_kernel(
@@ -105,7 +106,12 @@ def tile_list_echo_load_traits_kernel(
         n_rows = H_PASSES * len(vecs)
         cols = keep.tile([P, n_rows * PACK], F32, name="cols")
         nc.vector.tensor_copy(cols[:].rearrange("p (r i) -> p i r", i=PACK), turned[:, :, 0:n_rows])
-        last_cols = keep.tile([P, 2], F32, name="last_cols", tag="late")
+        last_b1 = []
+        for b in range(H_PASSES):
+            t = keep.tile([P, 1], F32, name="last_b1_%d" % b, tag="after_h%d" % b)
+            nc.vector.tensor_copy(t[:], turned[:, 2 + b, b : b + 1])
+            last_b1.append(t)
+        last_cols = keep.tile([P, 2], F32, name="last_cols", tag="after_look")
         nc.vector.tensor_copy(last_cols[:], turned[:, PACK - 1, 3:6:2])
         ov_cols = keep.tile([P, 4], F32, name="ov_cols")
         nc.vector.tensor_copy(ov_cols[:], turned_ov[:, 16:20])
@@ -113,6 +119,16 @@ def tile_list_echo_load_traits_kernel(
         def col(v, b, i0, i1):
             c = (H_PASSES * v + b) * PACK
             return cols[:, c + i0 : c + i1]
+
+        gain_m = keep.tile([P, H_PASSES * PACK], F32, name="gain_m")
+        nc.vector.tensor_scalar(gain_m[:], col(4, 0, 0, H_PASSES * PACK), float(M), None, ALU.mult)
+        openings = {}
+        for b in range(H_PASSES):
+            for i in range(PACK):
+                openings[b, i] = keep.tile([P, ROW], F32, name="opening%d%d" % (b, i))
+                nc.vector.tensor_scalar(
+                    openings[b, i][:, M:ROW], col(3, b, i, i + 1).to_broadcast([P, 2]), float(HALF), None, ALU.mult
+                )
 
         v_sc = keep.tile([P, S], U8, name="v_sc", align_bytes=64)
         v_words = []
@@ -126,14 +142,14 @@ def tile_list_echo_load_traits_kernel(
         w_codes = {}
         w_sc = {}
 
-        def weave_w1(engine_copy, b, a, i0, i1):
+        def weave_w1(engine_copy, b, a, i0, i1, m0=0, m1=P):
             if (b, a) not in w_bf:
                 w_bf[b, a] = ring.tile([P, PACK, P, PACK], BF16, name="w_bf", align_bytes=64)
                 w_codes[b, a] = keep.tile([P, SPAN], U32, name="wc%d%d" % (b, a), align_bytes=64)
                 w_sc[b, a] = keep.tile([P, SPAN], U8, name="ws%d%d" % (b, a), align_bytes=64)
             engine_copy(
-                w_bf[b, a][:, i0:i1, :, :].rearrange("p i m j -> p m j i"),
-                raw[b, a][:].rearrange("p j (m i) -> p m j i", i=PACK)[:, :, :, i0:i1],
+                w_bf[b, a][:, i0:i1, m0:m1, :].rearrange("p i m j -> p m j i"),
+                raw[b, a][:].rearrange("p j (m i) -> p m j i", i=PACK)[:, m0:m1, :, i0:i1],
             )
 
         def quant_w1(b, a, i0, i1):
@@ -165,47 +181,55 @@ def tile_list_echo_load_traits_kernel(
             h[b, i] = keep.tile([P, S], F32, name="h%d%d" % (b, i))
             for u in range(2):
                 dst = h[b, i][:, u * BANK : (u + 1) * BANK]
-                if (b, i) in SCALAR_EVAC:
-                    nc.scalar.activation(dst, acc_banks[b, i, u][:], ACT.Identity, bias=col(0, b, i, i + 1))
+                bias = last_b1[b][:] if i == 2 + b else col(0, b, i, i + 1)
+                if (b, i, u) in SCALAR_EVAC:
+                    nc.scalar.activation(dst, acc_banks[b, i, u][:], ACT.Identity, bias=bias)
                 else:
-                    nc.vector.tensor_scalar(dst, acc_banks[b, i, u][:], col(0, b, i, i + 1), None, ALU.add)
+                    nc.vector.tensor_scalar(dst, acc_banks[b, i, u][:], bias, None, ALU.add)
 
         sums = [keep.tile([P, PACK], F32, name="sums%d" % b) for b in range(H_PASSES)]
-        picked0 = keep.tile([P, PACK, M], F32, name="picked0", tag="raw00")
+        picked0 = [
+            keep.tile([P, 2, M], F32, name="picked00", tag="raw00"),
+            keep.tile([P, 2, M], F32, name="picked01", tag="after_h0"),
+        ]
         picked1 = [
-            keep.tile([P, PACK, HALF], F32, name="picked10", tag="raw01"),
-            keep.tile([P, PACK, HALF], F32, name="picked11", tag="late"),
+            keep.tile([P, 2, HALF], F32, name="picked10", tag="raw01"),
+            keep.tile([P, 2, HALF], F32, name="picked11", tag="after_h1"),
+            keep.tile([P, PACK, HALF], F32, name="picked12", tag="after_look"),
         ]
 
         def picked(b, i, m0, m1):
             if b == 0:
-                return picked0[:, i, m0:m1]
-            return picked1[m0 // HALF][:, i, :]
-
-
-        openings = {}
+                return picked0[i // 2][:, i % 2, m0:m1]
+            if m0 == 0:
+                return picked1[i // 2][:, i % 2, :]
+            return picked1[2][:, i, :]
 
         def look(b, i):
-            opening = ring.tile([P, M], F32, name="opening", bufs=8)
             nc.scalar.activation(
-                opening[:],
+                openings[b, i][:, 0:M],
                 h[b, i][:].indirect(idx2[:]),
                 ACT.Sigmoid,
-                bias=last_cols[:, 1:2] if (b, i) == (1, 3) else col(2, b, i, i + 1),
-                scale=last_cols[:, 0:1] if (b, i) == (1, 3) else col(1, b, i, i + 1),
+                bias=last_cols[:, 1:2] if (b, i) == (1, PACK - 1) else col(2, b, i, i + 1),
+                scale=last_cols[:, 0:1] if (b, i) == (1, PACK - 1) else col(1, b, i, i + 1),
             )
-            openings[b, i] = opening
 
         pair_sums = {}
 
         def row_sum(b, i):
-            if b not in pair_sums:
-                pair_sums[b] = keep.tile([P, PACK, HALF], F32, name="pair_sums%d" % b, tag="raw1%d" % (2 - b))
+            if (b, i) == (1, PACK - 1):
+                pairs = keep.tile([P, ROW // 2], F32, name="pairs13", tag="y_bf0", align_bytes=64)[:]
+            else:
+                if b not in pair_sums:
+                    pair_sums[b] = keep.tile(
+                        [P, PACK - b, ROW // 2], F32, name="pair_sums%d" % b, tag="raw1%d" % (2 - b)
+                    )
+                pairs = pair_sums[b][:, i, :]
             nc.vector.scalar_tensor_tensor(
-                pair_sums[b][:, i, :],
-                openings[b, i][:, 0:HALF],
+                pairs,
+                openings[b, i][:, 0 : ROW // 2],
                 1.0,
-                openings[b, i][:, HALF:M],
+                openings[b, i][:, ROW // 2 : ROW],
                 ALU.mult,
                 ALU.add,
                 accum_out=sums[b][:, i : i + 1],
@@ -216,47 +240,37 @@ def tile_list_echo_load_traits_kernel(
                 picked(b, i, m0, m1), h[b, i][:].indirect(idx2[:, m0 // 16 : m1 // 16]), ACT.Copy
             )
 
-        factor = {}
+        inv = [keep.tile([P, PACK], F32, name="inv%d" % b) for b in range(H_PASSES)]
+        factor0 = keep.tile([P, PACK], F32, name="factor0")
 
-        def make_factor(b):
-            load = keep.tile([P, PACK], F32, name="load%d" % b)
-            nc.vector.scalar_tensor_tensor(load[:], sums[b][:], 1.0 / M, col(3, b, 0, PACK), ALU.mult, ALU.add)
-            inv = keep.tile([P, PACK], F32, name="inv%d" % b)
-            nc.vector.reciprocal(inv[:], load[:])
-            factor[b] = keep.tile([P, PACK], F32, name="factor%d" % b)
-            nc.vector.tensor_tensor(factor[b][:], inv[:], col(4, b, 0, PACK), ALU.mult)
+        def invert(b, i0, i1):
+            nc.vector.reciprocal(inv[b][:, i0:i1], sums[b][:, i0:i1])
 
-        y_rows = [keep.tile([P, PACK, M], BF16, name="y_rows%d" % b) for b in range(H_PASSES)]
-        y_bf = [keep.tile([P, M, PACK], BF16, name="y_bf%d" % b, align_bytes=64) for b in range(H_PASSES)]
+        y_rows0 = keep.tile([P, PACK, M], BF16, name="y_rows0")
+        y_rows1 = keep.tile([P, PACK, HALF], BF16, name="y_rows1")
         y_codes = [keep.tile([P, M], U32, name="y_codes%d" % b, align_bytes=64) for b in range(H_PASSES)]
         y_sc = [keep.tile([P, M], U8, name="y_sc%d" % b, align_bytes=64) for b in range(H_PASSES)]
 
-        def scale_y(b, i, m0, m1):
+        def scale_y(dst, i, m0, m1):
             nc.vector.tensor_scalar(
-                y_rows[b][:, i, m0:m1], picked(b, i, m0, m1), factor[b][:, i : i + 1], None, ALU.mult
+                dst, picked(1, i, m0, m1), inv[1][:, i : i + 1], gain_m[:, PACK + i : PACK + i + 1], ALU.mult, ALU.mult
             )
 
-        def scale_y_pool(b, i):
+        def scale_y_pool(i):
             nc.gpsimd.tensor_scalar(
-                y_rows[b][:, i, :], picked(b, i, 0, M), factor[b][:, i : i + 1], 0.0, ALU.mult, ALU.add
+                y_rows0[:, i, :], picked(0, i, 0, M), factor0[:, i : i + 1], 0.0, ALU.mult, ALU.add
             )
 
-        def scale_y_scalar(b, i, m0, m1):
-            nc.scalar.activation(
-                y_rows[b][:, i, m0:m1], picked(b, i, m0, m1), ACT.Copy, scale=factor[b][:, i : i + 1]
-            )
-
-        def weave_y(b, m0, m1):
+        def weave_y(dst, src):
             nc.vector.tensor_copy(
-                y_bf[b][:, m0:m1, :].rearrange("p (c u) i -> p c i u", u=4),
-                y_rows[b][:, :, m0:m1].rearrange("p i (c u) -> p c i u", u=4),
+                dst.rearrange("p (c u) i -> p c i u", u=4), src.rearrange("p i (c u) -> p c i u", u=4)
             )
 
-        def quant_y(b, m0, m1):
+        def quant_y(src, b, m0, m1):
             nc.vector.quantize_mx(
                 out=y_codes[b][:, m0:m1].bitcast(FP8X4),
                 scales=y_sc[b][:, m0:m1],
-                in_=y_bf[b][:, m0:m1, :].rearrange("p m i -> p (m i)"),
+                in_=src[:].rearrange("p m i -> p (m i)"),
             )
 
         z_banks = {}
@@ -307,24 +321,24 @@ def tile_list_echo_load_traits_kernel(
         mm1(0, last, 3)
         evac(0, 0)
         look(0, 0)
-        evac(0, 1)
         pick(0, 0, 0, M)
-        weave_w1(nc.vector.tensor_copy, 1, 0, 0, PACK)
+        evac(0, 1)
         look(0, 1)
         pick(0, 1, 0, M)
+        weave_w1(nc.vector.tensor_copy, 1, 0, 0, PACK)
         evac(0, 2)
-        quant_w1(1, 0, 0, PACK)
-        weave_w1(nc.vector.tensor_copy, 1, 1, 0, PACK)
         look(0, 2)
+        quant_w1(1, 0, 0, PACK)
+        evac(0, 3)
+        look(0, 3)
         pick(0, 2, 0, M)
+        pick(0, 3, 0, M)
+        weave_w1(nc.vector.tensor_copy, 1, 1, 0, PACK)
+        weave_w1(nc.vector.tensor_copy, 1, 2, 0, PACK)
         quant_w1(1, 1, 0, PACK)
         for i in range(2):
             for a in range(last):
                 mm1(1, a, i)
-        weave_w1(nc.vector.tensor_copy, 1, last, 0, PACK)
-        evac(0, 3)
-        look(0, 3)
-        pick(0, 3, 0, M)
         quant_w1(1, last, 0, 2)
         mm1(1, last, 0)
         mm1(1, last, 1)
@@ -332,41 +346,46 @@ def tile_list_echo_load_traits_kernel(
         for i in range(2, PACK):
             for a in range(K_PASSES):
                 mm1(1, a, i)
-        for i in range(PACK - 1):
-            row_sum(0, i)
-        evac(1, 0)
-        look(1, 0)
-        pick(1, 0, 0, HALF)
-        row_sum(0, PACK - 1)
-        make_factor(0)
         for i in range(PACK):
-            scale_y_pool(0, i)
-        for i in range(1, PACK):
+            row_sum(0, i)
+        invert(0, 0, PACK)
+        nc.vector.tensor_tensor(factor0[:], inv[0][:], gain_m[:, 0:PACK], ALU.mult)
+        for i in range(PACK):
+            scale_y_pool(i)
+        for i in range(PACK):
             evac(1, i)
             look(1, i)
+            if i < 2:
+                pick(1, i, 0, HALF)
+        for i in range(2, PACK):
             pick(1, i, 0, HALF)
         for i in range(PACK):
             pick(1, i, HALF, M)
-        row_sum(1, 0)
-        weave_y(0, 0, M)
-        row_sum(1, 1)
-        quant_y(0, 0, M)
-        for i in range(2, PACK):
+        y_bf0 = keep.tile([P, M, PACK], BF16, name="y_bf0", tag="y_bf0", align_bytes=64)
+        weave_y(y_bf0[:], y_rows0[:])
+        for i in range(PACK - 1):
             row_sum(1, i)
+        quant_y(y_bf0, 0, 0, M)
         mm2(0, 0)
         mm2(0, 1)
-        make_factor(1)
-        for i in range(PACK):
-            scale_y(1, i, 0, HALF)
-        weave_y(1, 0, HALF)
-        scale_y(1, 0, HALF, M)
-        quant_y(1, 0, HALF)
+        invert(1, 0, PACK - 1)
+        row_sum(1, PACK - 1)
+        scale_y(y_rows1[:, 0, :], 0, 0, HALF)
+        invert(1, PACK - 1, PACK)
+        for i in range(1, PACK):
+            scale_y(y_rows1[:, i, :], i, 0, HALF)
+        y_bf1 = keep.tile([P, HALF, PACK], BF16, name="y_bf10", tag="y_bf1", align_bytes=64)
+        weave_y(y_bf1[:], y_rows1[:])
+        y_rows2 = keep.tile([P, 2, HALF], BF16, name="y_rows2", tag="after_h1")
+        for i in range(2):
+            scale_y(y_rows2[:, i, :], i, HALF, M)
+        quant_y(y_bf1, 1, 0, HALF)
         mm2(1, 0)
-        scale_y(1, 1, HALF, M)
-        scale_y_scalar(1, 2, HALF, M)
-        scale_y_scalar(1, 3, HALF, M)
-        weave_y(1, HALF, M)
-        quant_y(1, HALF, M)
+        y_bf1 = keep.tile([P, HALF, PACK], BF16, name="y_bf11", tag="y_bf1", align_bytes=64)
+        weave_y(y_bf1[:, :, 0:2], y_rows2[:])
+        for i in range(2, PACK):
+            scale_y(y_bf1[:, :, i], i, HALF, M)
+        quant_y(y_bf1, 1, HALF, M)
         mm2(1, 1)
         finish(0, [0, 1, 2, 3])
         finish(1, [1, 3])

from contextlib import ExitStack

import concourse.mybir as mybir
from concourse.masks import make_identity

F32 = mybir.dt.float32
BF16 = mybir.dt.bfloat16
I32 = mybir.dt.int32
U32 = mybir.dt.uint32
U16 = mybir.dt.uint16
U8 = mybir.dt.uint8
FP8X4 = mybir.dt.float8_e4m3fn_x4
FP4X4 = mybir.dt.float4_e2m1fn_x4
ACT = mybir.ActivationFunctionType
ALU = mybir.AluOpType

K, H, N, T, S, M = 1536, 1024, 512, 4096, 1024, 512
P = 128
PACK = 4
SPAN = P * PACK
K_PASSES = K // SPAN
H_PASSES = H // SPAN
BANK = 512
HALF = M // 2

FLOPS = 2 * K * H * S + 2 * H * N * M

SCALAR_EVAC = [(0, 3, 0), (0, 3, 1)]
ROW = M + 2


def tile_list_echo_load_traits_kernel(
    tc, tab_words, tab_scales, w1, b1, sc, th, base, gain, w4_words, w4_scales, ov, offs, offs2, out
):
    nc = tc.nc
    with ExitStack() as ctx:
        keep = ctx.enter_context(tc.tile_pool(name="keep", bufs=1))
        ring = ctx.enter_context(tc.tile_pool(name="ring", bufs=3))
        psum = ctx.enter_context(tc.psum_pool(name="psum", bufs=1))

        def bank(n, shape):
            return psum.tile(shape, F32, name="bank%d" % n, tag="bank%d" % n)

        idx = keep.tile([P, S // 16], U16, name="idx")
        nc.sync.dma_start(idx[:], offs)

        tab_sc = keep.tile([P, T], U8, name="tab_sc", align_bytes=64)
        nc.vector.memset(tab_sc[:].bitcast(I32), 0)
        rows = keep.tile([P, SPAN], F32, name="rows")
        nc.vector.memset(rows[:], 0.0)
        w4_sc = keep.tile([P, H_PASSES, N], U8, name="w4_sc", align_bytes=64)
        nc.vector.memset(w4_sc[:].bitcast(I32), 0)

        ident = keep.tile([P, P], F32, name="ident")
        make_identity(nc, ident[:])
        for q in range(4):
            nc.gpsimd.dma_start(
                tab_sc[32 * q : 32 * q + 4 * K_PASSES, :].bitcast(I32),
                tab_scales[:, 4 * q : 4 * q + 4, :].bitcast(I32),
            )

        vecs = [b1, sc, th, base, gain]
        for v, vec in enumerate(vecs):
            nc.scalar.dma_start(
                rows[H_PASSES * v : H_PASSES * (v + 1), :], vec.rearrange("(b c) -> b c", b=H_PASSES)
            )
        nc.scalar.dma_start(rows[16:20, 0:P], ov.rearrange("(c p) -> c p", p=P))

        tab = []
        raw = {}

        def load_tab(a):
            t = keep.tile([P, T], I32, name="tab%d" % a)
            nc.sync.dma_start(t[:], tab_words[a].rearrange("p t i -> p (t i)").bitcast(I32))
            tab.append(t)

        def load_w1(b, a):
            t = keep.tile([P, PACK, SPAN], F32, name="raw%d%d" % (b, a), tag="raw%d%d" % (b, a))
            nc.sync.dma_start(
                t[:],
                w1[a * SPAN : (a + 1) * SPAN, b * SPAN : (b + 1) * SPAN].rearrange("(p j) c -> p j c", j=PACK),
            )
            raw[b, a] = t

        for a in range(K_PASSES):
            load_tab(a)
            load_w1(0, a)
        idx2 = keep.tile([P, M // 16], U16, name="idx2")
        nc.sync.dma_start(idx2[:], offs2)
        for a in range(K_PASSES):
            load_w1(1, a)
        w4 = keep.tile([P, H_PASSES, 2 * N], U8, name="w4", align_bytes=64)
        nc.sync.dma_start(w4[:].bitcast(I32), w4_words.rearrange("a p n -> p a n").bitcast(I32))

        for q in range(4):
            nc.sync.dma_start(
                w4_sc[32 * q : 32 * q + 4, :, :].bitcast(I32),
                w4_scales[:, 4 * q : 4 * q + 4, :].rearrange("a r n -> r a n").bitcast(I32),
            )

        turned = bank(0, [P, PACK, P])
        for i in range(PACK):
            nc.tensor.transpose(turned[:, i, :], rows[:, i:SPAN:PACK], ident[:])
        turned_ov = bank(1, [P, P])
        nc.tensor.transpose(turned_ov[:], rows[:, 0:P], ident[:])
        n_rows = H_PASSES * len(vecs)
        cols = keep.tile([P, n_rows * PACK], F32, name="cols")
        nc.vector.tensor_copy(cols[:].rearrange("p (r i) -> p i r", i=PACK), turned[:, :, 0:n_rows])
        last_b1 = []
        for b in range(H_PASSES):
            t = keep.tile([P, 1], F32, name="last_b1_%d" % b, tag="after_h%d" % b)
            nc.vector.tensor_copy(t[:], turned[:, 2 + b, b : b + 1])
            last_b1.append(t)
        last_cols = keep.tile([P, 2], F32, name="last_cols", tag="after_look")
        nc.vector.tensor_copy(last_cols[:], turned[:, PACK - 1, 3:6:2])
        ov_cols = keep.tile([P, 4], F32, name="ov_cols")
        nc.vector.tensor_copy(ov_cols[:], turned_ov[:, 16:20])

        def col(v, b, i0, i1):
            c = (H_PASSES * v + b) * PACK
            return cols[:, c + i0 : c + i1]

        gain_m = keep.tile([P, H_PASSES * PACK], F32, name="gain_m")
        nc.vector.tensor_scalar(gain_m[:], col(4, 0, 0, H_PASSES * PACK), float(M), None, ALU.mult)
        openings = {}
        for b in range(H_PASSES):
            for i in range(PACK):
                openings[b, i] = keep.tile([P, ROW], F32, name="opening%d%d" % (b, i))
                nc.vector.tensor_scalar(
                    openings[b, i][:, M:ROW], col(3, b, i, i + 1).to_broadcast([P, 2]), float(HALF), None, ALU.mult
                )

        v_sc = keep.tile([P, S], U8, name="v_sc", align_bytes=64)
        v_words = []

        def gather_tab(a):
            t = keep.tile([P, S], U32, name="v%d" % a, align_bytes=64)
            nc.vector.tensor_copy(t[:], tab[a][:].bitcast(U32).indirect(idx[:]))
            v_words.append(t)

        w_bf = {}
        w_codes = {}
        w_sc = {}

        def weave_w1(engine_copy, b, a, i0, i1, m0=0, m1=P):
            if (b, a) not in w_bf:
                w_bf[b, a] = ring.tile([P, PACK, P, PACK], BF16, name="w_bf", align_bytes=64)
                w_codes[b, a] = keep.tile([P, SPAN], U32, name="wc%d%d" % (b, a), align_bytes=64)
                w_sc[b, a] = keep.tile([P, SPAN], U8, name="ws%d%d" % (b, a), align_bytes=64)
            engine_copy(
                w_bf[b, a][:, i0:i1, m0:m1, :].rearrange("p i m j -> p m j i"),
                raw[b, a][:].rearrange("p j (m i) -> p m j i", i=PACK)[:, m0:m1, :, i0:i1],
            )

        def quant_w1(b, a, i0, i1):
            nc.vector.quantize_mx(
                out=w_codes[b, a][:, i0 * P : i1 * P].bitcast(FP8X4),
                scales=w_sc[b, a][:, i0 * P : i1 * P],
                in_=w_bf[b, a][:, i0:i1, :, :].rearrange("p i m j -> p (i m j)"),
            )

        acc_banks = {}

        def mm1(b, a, i):
            for u in range(2):
                if a == 0:
                    acc_banks[b, i, u] = bank(2 * i + u, [P, BANK])
                nc.tensor.matmul_mx(
                    out=acc_banks[b, i, u][:],
                    lhsT=w_codes[b, a][:, i * P : (i + 1) * P].bitcast(FP8X4),
                    lhsT_scale=w_sc[b, a][:, i * P : (i + 1) * P],
                    rhs=v_words[a][:, u * BANK : (u + 1) * BANK].bitcast(FP8X4),
                    rhs_scale=v_sc[4 * a : P, u * BANK : (u + 1) * BANK],
                    start=(a == 0),
                    stop=(a == K_PASSES - 1),
                )

        h = {}

        def evac(b, i):
            h[b, i] = keep.tile([P, S], F32, name="h%d%d" % (b, i))
            for u in range(2):
                dst = h[b, i][:, u * BANK : (u + 1) * BANK]
                bias = last_b1[b][:] if i == 2 + b else col(0, b, i, i + 1)
                if (b, i, u) in SCALAR_EVAC:
                    nc.scalar.activation(dst, acc_banks[b, i, u][:], ACT.Identity, bias=bias)
                else:
                    nc.vector.tensor_scalar(dst, acc_banks[b, i, u][:], bias, None, ALU.add)

        sums = [keep.tile([P, PACK], F32, name="sums%d" % b) for b in range(H_PASSES)]
        picked0 = [
            keep.tile([P, 2, M], F32, name="picked00", tag="raw00"),
            keep.tile([P, 2, M], F32, name="picked01", tag="after_h0"),
        ]
        picked1 = [
            keep.tile([P, 2, HALF], F32, name="picked10", tag="raw01"),
            keep.tile([P, 2, HALF], F32, name="picked11", tag="after_h1"),
            keep.tile([P, PACK, HALF], F32, name="picked12", tag="after_look"),
        ]

        def picked(b, i, m0, m1):
            if b == 0:
                return picked0[i // 2][:, i % 2, m0:m1]
            if m0 == 0:
                return picked1[i // 2][:, i % 2, :]
            return picked1[2][:, i, :]

        def look(b, i):
            nc.scalar.activation(
                openings[b, i][:, 0:M],
                h[b, i][:].indirect(idx2[:]),
                ACT.Sigmoid,
                bias=last_cols[:, 1:2] if (b, i) == (1, PACK - 1) else col(2, b, i, i + 1),
                scale=last_cols[:, 0:1] if (b, i) == (1, PACK - 1) else col(1, b, i, i + 1),
            )

        pair_sums = {}

        def row_sum(b, i):
            if (b, i) == (1, PACK - 1):
                pairs = keep.tile([P, ROW // 2], F32, name="pairs13", tag="y_bf0", align_bytes=64)[:]
            else:
                if b not in pair_sums:
                    pair_sums[b] = keep.tile(
                        [P, PACK - b, ROW // 2], F32, name="pair_sums%d" % b, tag="raw1%d" % (2 - b)
                    )
                pairs = pair_sums[b][:, i, :]
            nc.vector.scalar_tensor_tensor(
                pairs,
                openings[b, i][:, 0 : ROW // 2],
                1.0,
                openings[b, i][:, ROW // 2 : ROW],
                ALU.mult,
                ALU.add,
                accum_out=sums[b][:, i : i + 1],
            )

        def pick(b, i, m0, m1):
            nc.scalar.activation(
                picked(b, i, m0, m1), h[b, i][:].indirect(idx2[:, m0 // 16 : m1 // 16]), ACT.Copy
            )

        inv = [keep.tile([P, PACK], F32, name="inv%d" % b) for b in range(H_PASSES)]
        factor0 = keep.tile([P, PACK], F32, name="factor0")

        def invert(b, i0, i1):
            nc.vector.reciprocal(inv[b][:, i0:i1], sums[b][:, i0:i1])

        y_rows0 = keep.tile([P, PACK, M], BF16, name="y_rows0")
        y_rows1 = keep.tile([P, PACK, HALF], BF16, name="y_rows1")
        y_codes = [keep.tile([P, M], U32, name="y_codes%d" % b, align_bytes=64) for b in range(H_PASSES)]
        y_sc = [keep.tile([P, M], U8, name="y_sc%d" % b, align_bytes=64) for b in range(H_PASSES)]

        def scale_y(dst, i, m0, m1):
            nc.vector.tensor_scalar(
                dst, picked(1, i, m0, m1), inv[1][:, i : i + 1], gain_m[:, PACK + i : PACK + i + 1], ALU.mult, ALU.mult
            )

        def scale_y_pool(i):
            nc.gpsimd.tensor_scalar(
                y_rows0[:, i, :], picked(0, i, 0, M), factor0[:, i : i + 1], 0.0, ALU.mult, ALU.add
            )

        def weave_y(dst, src):
            nc.vector.tensor_copy(
                dst.rearrange("p (c u) i -> p c i u", u=4), src.rearrange("p i (c u) -> p c i u", u=4)
            )

        def quant_y(src, b, m0, m1):
            nc.vector.quantize_mx(
                out=y_codes[b][:, m0:m1].bitcast(FP8X4),
                scales=y_sc[b][:, m0:m1],
                in_=src[:].rearrange("p m i -> p (m i)"),
            )

        z_banks = {}

        def mm2(b, u):
            for c in range(4):
                if b == 0:
                    z_banks[u, c] = bank(4 * u + c, [P, HALF])
                nc.tensor.matmul_mx(
                    out=z_banks[u, c][:],
                    lhsT=w4[:, b, 2 * P * c : 2 * P * (c + 1)].bitcast(FP4X4),
                    lhsT_scale=w4_sc[:, b, P * c : P * (c + 1)],
                    rhs=y_codes[b][:, u * HALF : (u + 1) * HALF].bitcast(FP8X4),
                    rhs_scale=y_sc[b][:, u * HALF : (u + 1) * HALF],
                    start=(b == 0),
                    stop=(b == H_PASSES - 1),
                )

        out_v = out.rearrange("(c p) m -> p c m", p=P)

        def finish(u, on_scalar):
            for c in range(4):
                res = keep.tile([P, HALF], F32, name="res%d%d" % (u, c))
                if c in on_scalar:
                    nc.scalar.activation(res[:], z_banks[u, c][:], ACT.Copy, scale=ov_cols[:, c : c + 1])
                else:
                    nc.vector.tensor_scalar(res[:], z_banks[u, c][:], ov_cols[:, c : c + 1], None, ALU.mult)
                nc.sync.dma_start(out_v[:, c, u * HALF : (u + 1) * HALF], res[:])

        gather_tab(0)
        nc.vector.tensor_copy(v_sc[:], tab_sc[:].indirect(idx[:]))
        for a in range(K_PASSES - 1):
            if a > 0:
                gather_tab(a)
            weave_w1(nc.scalar.copy, 0, a, 0, PACK)
            quant_w1(0, a, 0, PACK)
            for i in range(PACK):
                mm1(0, a, i)
        last = K_PASSES - 1
        gather_tab(last)
        weave_w1(nc.vector.tensor_copy, 0, last, 0, 2)
        weave_w1(nc.scalar.copy, 0, last, 2, 4)
        quant_w1(0, last, 0, 2)
        mm1(0, last, 0)
        mm1(0, last, 1)
        quant_w1(0, last, 2, 4)
        mm1(0, last, 2)
        mm1(0, last, 3)
        evac(0, 0)
        look(0, 0)
        pick(0, 0, 0, M)
        evac(0, 1)
        look(0, 1)
        pick(0, 1, 0, M)
        weave_w1(nc.vector.tensor_copy, 1, 0, 0, PACK)
        evac(0, 2)
        look(0, 2)
        quant_w1(1, 0, 0, PACK)
        evac(0, 3)
        look(0, 3)
        pick(0, 2, 0, M)
        pick(0, 3, 0, M)
        weave_w1(nc.vector.tensor_copy, 1, 1, 0, PACK)
        weave_w1(nc.vector.tensor_copy, 1, 2, 0, PACK)
        quant_w1(1, 1, 0, PACK)
        for i in range(2):
            for a in range(last):
                mm1(1, a, i)
        quant_w1(1, last, 0, 2)
        mm1(1, last, 0)
        mm1(1, last, 1)
        quant_w1(1, last, 2, 4)
        for i in range(2, PACK):
            for a in range(K_PASSES):
                mm1(1, a, i)
        for i in range(PACK):
            row_sum(0, i)
        invert(0, 0, PACK)
        nc.vector.tensor_tensor(factor0[:], inv[0][:], gain_m[:, 0:PACK], ALU.mult)
        for i in range(PACK):
            scale_y_pool(i)
        for i in range(PACK):
            evac(1, i)
            look(1, i)
            if i < 2:
                pick(1, i, 0, HALF)
        for i in range(2, PACK):
            pick(1, i, 0, HALF)
        for i in range(PACK):
            pick(1, i, HALF, M)
        y_bf0 = keep.tile([P, M, PACK], BF16, name="y_bf0", tag="y_bf0", align_bytes=64)
        weave_y(y_bf0[:], y_rows0[:])
        for i in range(PACK - 1):
            row_sum(1, i)
        quant_y(y_bf0, 0, 0, M)
        mm2(0, 0)
        mm2(0, 1)
        invert(1, 0, PACK - 1)
        row_sum(1, PACK - 1)
        scale_y(y_rows1[:, 0, :], 0, 0, HALF)
        invert(1, PACK - 1, PACK)
        for i in range(1, PACK):
            scale_y(y_rows1[:, i, :], i, 0, HALF)
        y_bf1 = keep.tile([P, HALF, PACK], BF16, name="y_bf10", tag="y_bf1", align_bytes=64)
        weave_y(y_bf1[:], y_rows1[:])
        y_rows2 = keep.tile([P, 2, HALF], BF16, name="y_rows2", tag="after_h1")
        for i in range(2):
            scale_y(y_rows2[:, i, :], i, HALF, M)
        quant_y(y_bf1, 1, 0, HALF)
        mm2(1, 0)
        y_bf1 = keep.tile([P, HALF, PACK], BF16, name="y_bf11", tag="y_bf1", align_bytes=64)
        weave_y(y_bf1[:, :, 0:2], y_rows2[:])
        for i in range(2, PACK):
            scale_y(y_bf1[:, :, i], i, HALF, M)
        quant_y(y_bf1, 1, HALF, M)
        mm2(1, 1)
        finish(0, [0, 1, 2, 3])
        finish(1, [1, 3])
